import numpy as np, ml_dtypes
CORES = [6,22,38,54,70,86,102,118,134,150,166,182,198,214,230,246]
N = 16
def setup_inputs(rng):
    return {"x": rng.standard_normal((N, 128, 4096), dtype=np.float32).astype(ml_dtypes.bfloat16)}
def reference(x):
    s = x.sum(axis=0, dtype=np.float64).astype(x.dtype)
    return {"y": np.broadcast_to(s, (N,) + s.shape)}

@@ -1,0 +1,85 @@
+from concourse.bass import DstId, RemoteDMATransfer
+
+R = 16
+CHUNKS = [
+    (64, None, 0, 4),
+    (64, None, 0, 0),
+    (64, None, 0, 5),
+    (64, None, 0, 1),
+]
+ORDER = [0, 1, 2, 3]
+MAXC = 8
+
+SCRATCH = {}
+for k in range(MAXC):
+    shape = [R, 128, CHUNKS[k][0]] if k < len(CHUNKS) else [1, 128, 2]
+    SCRATCH["xs%d" % k] = ("dram", shape, "bfloat16")
+    SCRATCH["ln%d" % k] = ("dram", shape, "bfloat16")
+SEMAPHORES = (["ld%d" % k for k in range(MAXC)] + ["hp%d" % k for k in range(MAXC)] + ["rs%d" % k for k in range(MAXC)]
+              + ["ag%d" % k for k in range(MAXC)] + ["sent", "st"])
+
+
+def rank_program(g, core, T, topo):
+    xs = [T.xs0, T.xs1, T.xs2, T.xs3, T.xs4, T.xs5, T.xs6, T.xs7]
+    ln = [T.ln0, T.ln1, T.ln2, T.ln3, T.ln4, T.ln5, T.ln6, T.ln7]
+    s = T.sem
+    ld = [s.ld0, s.ld1, s.ld2, s.ld3, s.ld4, s.ld5, s.ld6, s.ld7]
+    hp = [s.hp0, s.hp1, s.hp2, s.hp3, s.hp4, s.hp5, s.hp6, s.hp7]
+    rs = [s.rs0, s.rs1, s.rs2, s.rs3, s.rs4, s.rs5, s.rs6, s.rs7]
+    ag = [s.ag0, s.ag1, s.ag2, s.ag3, s.ag4, s.ag5, s.ag6, s.ag7]
+
+    pair, within = core // 16, core % 16
+    par, idx = within // 8, within % 8
+    base = pair * 16
+    row0 = [sum(c[0] for c in CHUNKS[:k]) // 2 for k in range(len(CHUNKS) + 1)]
+
+    def dst(d):
+        rid, pid = topo.addr(d, core)
+        return DstId(rid=rid, pnc=pid)
+
+    def scatter(k):
+        n, via, rpar, rcore = CHUNKS[k]
+        for half in range(2):
+            tr = []
+            for e in range(8):
+                j = (pair + half * 8 + e) % R
+                tr.append(RemoteDMATransfer(dst_ids=[dst(j * 16 + rpar * 8 + rcore)], dma_engine_mask=1 << e,
+                                            remote_sem=rs[k], src=xs[k][j], dst=ln[k][pair]))
+            g.remote_dma_fused(tr, local_sem=s.sent)
+        return 16
+
+    sent = 0
+    if par == 0 and idx == 6:
+        for k in ORDER:
+            g.dma_start(xs[k][:], T.x[row0[k]:row0[k + 1], :]).then_inc(ld[k], 16)
+        for k in ORDER:
+            n, via, rpar, rcore = CHUNKS[k]
+            g.wait_ge(ld[k], 16)
+            if via is None:
+                sent += scatter(k)
+            else:
+                tr = [RemoteDMATransfer(dst_ids=[dst(base + via)], dma_engine_mask=1 << j, remote_sem=hp[k],
+                                        src=xs[k][j], dst=xs[k][j]) for j in range(R)]
+                g.remote_dma_fused(tr, local_sem=s.sent)
+                sent += 16
+        for k in ORDER:
+            g.wait_ge(ag[k], 8 * R)
+            g.dma_start(T.y[row0[k]:row0[k + 1], :], ln[k][:]).then_inc(s.st, 16)
+        g.wait_ge(s.st, 16 * len(ORDER))
+        g.wait_ge(s.sent, sent)
+        return
+
+    for k in ORDER:
+        n, via, rpar, rcore = CHUNKS[k]
+        if par == 0 and via == idx:
+            g.wait_ge(hp[k], 16)
+            sent += scatter(k)
+        if par == rpar and idx == rcore:
+            g.wait_ge(rs[k], 16)
+            to = [(pair + t) % R for t in range(R)]
+            g.remote_dma_fused([RemoteDMATransfer(
+                dst_ids=[dst(i * 16 + 6) for i in to], dma_engine_mask=0xFF, remote_sem=ag[k],
+                srcs=[ln[k][r] for r in range(R)], dsts=[ln[k][pair] for i in to], alu_op=1)], local_sem=s.sent)
+            sent += 8
+    if sent:
+        g.wait_ge(s.sent, sent)

@@ -2,10 +2,10 @@ from concourse.bass import DstId, RemoteDMATransfer
 
 R = 16
 CHUNKS = [
-    (64, None, 0, 4),
     (64, None, 0, 0),
-    (64, None, 0, 5),
     (64, None, 0, 1),
+    (64, None, 0, 2),
+    (64, None, 0, 3),
 ]
 ORDER = [0, 1, 2, 3]
 MAXC = 8

@@ -2,13 +2,13 @@ from concourse.bass import DstId, RemoteDMATransfer
 
 R = 16
 CHUNKS = [
-    (64, None, 0, 0),
-    (64, None, 0, 1),
-    (64, None, 0, 2),
-    (64, None, 0, 3),
+    (68, None, 0, 0),
+    (68, None, 0, 1),
+    (66, None, 0, 2),
+    (54, None, 0, 3),
 ]
-ORDER = [0, 1, 2, 3]
-MAXC = 8
+ORDER = list(range(len(CHUNKS)))
+MAXC = 12
 
 SCRATCH = {}
 for k in range(MAXC):
@@ -20,13 +20,13 @@ SEMAPHORES = (["ld%d" % k for k in range(MAXC)] + ["hp%d" % k for k in range(MAX
 
 
 def rank_program(g, core, T, topo):
-    xs = [T.xs0, T.xs1, T.xs2, T.xs3, T.xs4, T.xs5, T.xs6, T.xs7]
-    ln = [T.ln0, T.ln1, T.ln2, T.ln3, T.ln4, T.ln5, T.ln6, T.ln7]
+    xs = [T.xs0, T.xs1, T.xs2, T.xs3, T.xs4, T.xs5, T.xs6, T.xs7, T.xs8, T.xs9, T.xs10, T.xs11]
+    ln = [T.ln0, T.ln1, T.ln2, T.ln3, T.ln4, T.ln5, T.ln6, T.ln7, T.ln8, T.ln9, T.ln10, T.ln11]
     s = T.sem
-    ld = [s.ld0, s.ld1, s.ld2, s.ld3, s.ld4, s.ld5, s.ld6, s.ld7]
-    hp = [s.hp0, s.hp1, s.hp2, s.hp3, s.hp4, s.hp5, s.hp6, s.hp7]
-    rs = [s.rs0, s.rs1, s.rs2, s.rs3, s.rs4, s.rs5, s.rs6, s.rs7]
-    ag = [s.ag0, s.ag1, s.ag2, s.ag3, s.ag4, s.ag5, s.ag6, s.ag7]
+    ld = [s.ld0, s.ld1, s.ld2, s.ld3, s.ld4, s.ld5, s.ld6, s.ld7, s.ld8, s.ld9, s.ld10, s.ld11]
+    hp = [s.hp0, s.hp1, s.hp2, s.hp3, s.hp4, s.hp5, s.hp6, s.hp7, s.hp8, s.hp9, s.hp10, s.hp11]
+    rs = [s.rs0, s.rs1, s.rs2, s.rs3, s.rs4, s.rs5, s.rs6, s.rs7, s.rs8, s.rs9, s.rs10, s.rs11]
+    ag = [s.ag0, s.ag1, s.ag2, s.ag3, s.ag4, s.ag5, s.ag6, s.ag7, s.ag8, s.ag9, s.ag10, s.ag11]
 
     pair, within = core // 16, core % 16
     par, idx = within // 8, within % 8

@@ -1,85 +1,56 @@
 from concourse.bass import DstId, RemoteDMATransfer
 
 R = 16
-CHUNKS = [
-    (68, None, 0, 0),
-    (68, None, 0, 1),
-    (66, None, 0, 2),
-    (54, None, 0, 3),
-]
-ORDER = list(range(len(CHUNKS)))
-MAXC = 12
+CHUNKS = [(68, 0), (68, 1), (66, 2), (54, 3)]
+NC = len(CHUNKS)
 
 SCRATCH = {}
-for k in range(MAXC):
-    shape = [R, 128, CHUNKS[k][0]] if k < len(CHUNKS) else [1, 128, 2]
-    SCRATCH["xs%d" % k] = ("dram", shape, "bfloat16")
-    SCRATCH["ln%d" % k] = ("dram", shape, "bfloat16")
-SEMAPHORES = (["ld%d" % k for k in range(MAXC)] + ["hp%d" % k for k in range(MAXC)] + ["rs%d" % k for k in range(MAXC)]
-              + ["ag%d" % k for k in range(MAXC)] + ["sent", "st"])
+for k in range(NC):
+    SCRATCH["xs%d" % k] = ("dram", [R, 128, CHUNKS[k][0]], "bfloat16")
+    SCRATCH["ln%d" % k] = ("dram", [R, 128, CHUNKS[k][0]], "bfloat16")
+SEMAPHORES = (["ld%d" % k for k in range(NC)] + ["rs%d" % k for k in range(NC)] + ["ag%d" % k for k in range(NC)]
+              + ["sent", "st"])
 
 
 def rank_program(g, core, T, topo):
-    xs = [T.xs0, T.xs1, T.xs2, T.xs3, T.xs4, T.xs5, T.xs6, T.xs7, T.xs8, T.xs9, T.xs10, T.xs11]
-    ln = [T.ln0, T.ln1, T.ln2, T.ln3, T.ln4, T.ln5, T.ln6, T.ln7, T.ln8, T.ln9, T.ln10, T.ln11]
+    xs = [T.xs0, T.xs1, T.xs2, T.xs3]
+    ln = [T.ln0, T.ln1, T.ln2, T.ln3]
     s = T.sem
-    ld = [s.ld0, s.ld1, s.ld2, s.ld3, s.ld4, s.ld5, s.ld6, s.ld7, s.ld8, s.ld9, s.ld10, s.ld11]
-    hp = [s.hp0, s.hp1, s.hp2, s.hp3, s.hp4, s.hp5, s.hp6, s.hp7, s.hp8, s.hp9, s.hp10, s.hp11]
-    rs = [s.rs0, s.rs1, s.rs2, s.rs3, s.rs4, s.rs5, s.rs6, s.rs7, s.rs8, s.rs9, s.rs10, s.rs11]
-    ag = [s.ag0, s.ag1, s.ag2, s.ag3, s.ag4, s.ag5, s.ag6, s.ag7, s.ag8, s.ag9, s.ag10, s.ag11]
+    ld = [s.ld0, s.ld1, s.ld2, s.ld3]
+    rs = [s.rs0, s.rs1, s.rs2, s.rs3]
+    ag = [s.ag0, s.ag1, s.ag2, s.ag3]
 
     pair, within = core // 16, core % 16
-    par, idx = within // 8, within % 8
-    base = pair * 16
-    row0 = [sum(c[0] for c in CHUNKS[:k]) // 2 for k in range(len(CHUNKS) + 1)]
+    row0 = [sum(c[0] for c in CHUNKS[:k]) // 2 for k in range(NC + 1)]
 
     def dst(d):
         rid, pid = topo.addr(d, core)
         return DstId(rid=rid, pnc=pid)
 
-    def scatter(k):
-        n, via, rpar, rcore = CHUNKS[k]
-        for half in range(2):
-            tr = []
-            for e in range(8):
-                j = (pair + half * 8 + e) % R
-                tr.append(RemoteDMATransfer(dst_ids=[dst(j * 16 + rpar * 8 + rcore)], dma_engine_mask=1 << e,
-                                            remote_sem=rs[k], src=xs[k][j], dst=ln[k][pair]))
-            g.remote_dma_fused(tr, local_sem=s.sent)
-        return 16
-
-    sent = 0
-    if par == 0 and idx == 6:
-        for k in ORDER:
+    if within == 6:
+        for k in range(NC):
             g.dma_start(xs[k][:], T.x[row0[k]:row0[k + 1], :]).then_inc(ld[k], 16)
-        for k in ORDER:
-            n, via, rpar, rcore = CHUNKS[k]
+        for k in range(NC):
             g.wait_ge(ld[k], 16)
-            if via is None:
-                sent += scatter(k)
-            else:
-                tr = [RemoteDMATransfer(dst_ids=[dst(base + via)], dma_engine_mask=1 << j, remote_sem=hp[k],
-                                        src=xs[k][j], dst=xs[k][j]) for j in range(R)]
+            for half in range(2):
+                tr = []
+                for e in range(8):
+                    j = (pair + half * 8 + e) % R
+                    tr.append(RemoteDMATransfer(dst_ids=[dst(j * 16 + CHUNKS[k][1])], dma_engine_mask=1 << e,
+                                                remote_sem=rs[k], src=xs[k][j], dst=ln[k][pair]))
                 g.remote_dma_fused(tr, local_sem=s.sent)
-                sent += 16
-        for k in ORDER:
+        for k in range(NC):
             g.wait_ge(ag[k], 8 * R)
             g.dma_start(T.y[row0[k]:row0[k + 1], :], ln[k][:]).then_inc(s.st, 16)
-        g.wait_ge(s.st, 16 * len(ORDER))
-        g.wait_ge(s.sent, sent)
+        g.wait_ge(s.st, 16 * NC)
+        g.wait_ge(s.sent, 16 * NC)
         return
 
-    for k in ORDER:
-        n, via, rpar, rcore = CHUNKS[k]
-        if par == 0 and via == idx:
-            g.wait_ge(hp[k], 16)
-            sent += scatter(k)
-        if par == rpar and idx == rcore:
-            g.wait_ge(rs[k], 16)
+    for k in range(NC):
+        if within == CHUNKS[k][1]:
+            g.wait_ge(rs[k], R)
             to = [(pair + t) % R for t in range(R)]
             g.remote_dma_fused([RemoteDMATransfer(
                 dst_ids=[dst(i * 16 + 6) for i in to], dma_engine_mask=0xFF, remote_sem=ag[k],
                 srcs=[ln[k][r] for r in range(R)], dsts=[ln[k][pair] for i in to], alu_op=1)], local_sem=s.sent)
-            sent += 8
-    if sent:
-        g.wait_ge(s.sent, sent)
+            g.wait_ge(s.sent, 8)

from concourse.bass import DstId, RemoteDMATransfer

R = 16
CHUNKS = [(68, 0), (68, 1), (66, 2), (54, 3)]
NC = len(CHUNKS)

SCRATCH = {}
for k in range(NC):
    SCRATCH["xs%d" % k] = ("dram", [R, 128, CHUNKS[k][0]], "bfloat16")
    SCRATCH["ln%d" % k] = ("dram", [R, 128, CHUNKS[k][0]], "bfloat16")
SEMAPHORES = (["ld%d" % k for k in range(NC)] + ["rs%d" % k for k in range(NC)] + ["ag%d" % k for k in range(NC)]
              + ["sent", "st"])


def rank_program(g, core, T, topo):
    xs = [T.xs0, T.xs1, T.xs2, T.xs3]
    ln = [T.ln0, T.ln1, T.ln2, T.ln3]
    s = T.sem
    ld = [s.ld0, s.ld1, s.ld2, s.ld3]
    rs = [s.rs0, s.rs1, s.rs2, s.rs3]
    ag = [s.ag0, s.ag1, s.ag2, s.ag3]

    pair, within = core // 16, core % 16
    row0 = [sum(c[0] for c in CHUNKS[:k]) // 2 for k in range(NC + 1)]

    def dst(d):
        rid, pid = topo.addr(d, core)
        return DstId(rid=rid, pnc=pid)

    if within == 6:
        for k in range(NC):
            g.dma_start(xs[k][:], T.x[row0[k]:row0[k + 1], :]).then_inc(ld[k], 16)
        for k in range(NC):
            g.wait_ge(ld[k], 16)
            for half in range(2):
                tr = []
                for e in range(8):
                    j = (pair + half * 8 + e) % R
                    tr.append(RemoteDMATransfer(dst_ids=[dst(j * 16 + CHUNKS[k][1])], dma_engine_mask=1 << e,
                                                remote_sem=rs[k], src=xs[k][j], dst=ln[k][pair]))
                g.remote_dma_fused(tr, local_sem=s.sent)
        for k in range(NC):
            g.wait_ge(ag[k], 8 * R)
            g.dma_start(T.y[row0[k]:row0[k + 1], :], ln[k][:]).then_inc(s.st, 16)
        g.wait_ge(s.st, 16 * NC)
        g.wait_ge(s.sent, 16 * NC)
        return

    for k in range(NC):
        if within == CHUNKS[k][1]:
            g.wait_ge(rs[k], R)
            to = [(pair + t) % R for t in range(R)]
            g.remote_dma_fused([RemoteDMATransfer(
                dst_ids=[dst(i * 16 + 6) for i in to], dma_engine_mask=0xFF, remote_sem=ag[k],
                srcs=[ln[k][r] for r in range(R)], dsts=[ln[k][pair] for i in to], alu_op=1)], local_sem=s.sent)
            g.wait_ge(s.sent, 8)
